import numpy as np
import ml_dtypes


def mxq(x, axis, fmt="e4m3"):
    dtype, down = {"e4m3": (ml_dtypes.float8_e4m3fn, 7), "e5m2": (ml_dtypes.float8_e5m2, 14)}[fmt]
    v = np.moveaxis(np.asarray(x, np.float32).astype(ml_dtypes.bfloat16).astype(np.float64), axis, -1)
    blocks = v.reshape(v.shape[:-1] + (-1, 32))
    amax = np.abs(blocks).max(-1, keepdims=True)
    byte = np.maximum(np.where(amax > 0, np.frexp(amax)[1] - 1 + 127, 0) - down, 1)
    scale = np.exp2(byte - 127.0)
    codes = (blocks / scale).astype(np.float32).astype(dtype).astype(np.float64)
    return np.moveaxis((codes * scale).reshape(v.shape), -1, axis)


WIDE = False


def mx_kscale(k):
    if not WIDE:
        return np.ones(k)
    levels = np.array([10, -10, 5, -5, 0])
    if k % 512:
        return np.exp2(np.random.permutation(np.resize(levels, k // 32))).repeat(32)
    a = np.empty((k // 512, 16))
    for p in range(k // 512):
        a[p, :8] = np.random.permutation(np.resize(levels, 8))
        for g in range(8):
            far = levels[np.abs(levels - a[p, g]) >= 10]
            a[p, g + 8] = far[np.random.randint(len(far))]
    return np.exp2(a.ravel()).repeat(32)


def f64(x):
    return np.asarray(x).astype(np.float64)


E2M1 = np.array([0.0, 0.5, 1.0, 1.5, 2.0, 3.0, 4.0, 6.0, -0.0, -0.5, -1.0, -1.5, -2.0, -3.0, -4.0, -6.0])


def pack_weight(w, fmt):
    k, n = w.shape
    w = f64(np.asarray(w, np.float32).astype(ml_dtypes.bfloat16)).reshape(k // 32, 32, n)
    amax = np.abs(w).max(1)
    if fmt == "e4m3":
        byte = np.frexp(amax)[1] - 1 + 127 - 7
    else:
        mant, ex = np.frexp(amax / 6.0)
        byte = np.where(mant > 0.5, ex, ex - 1) + 127
    byte = np.clip(np.where(amax > 0, byte, 1), 1, 254)
    scaled = (w * np.exp2(127.0 - byte)[:, None, :]).reshape(k, n).astype(np.float32)
    by_word = np.ascontiguousarray(scaled.reshape(k // 512, 128, 4, n).transpose(0, 1, 3, 2))
    if fmt == "e4m3":
        words = by_word.astype(ml_dtypes.float8_e4m3fn).view(np.uint8)
    else:
        c = by_word.astype(ml_dtypes.float4_e2m1fn).view(np.uint8) & 0xF
        words = (c[..., 0::2] | (c[..., 1::2] << 4)).reshape(k // 512, 128, 2 * n)
    return np.ascontiguousarray(words), np.ascontiguousarray(byte.astype(np.uint8).reshape(k // 512, 16, n))


def unpack_weight(words, scales, fmt):
    g, _, n = scales.shape
    words = np.ascontiguousarray(words).reshape(g, 128, n, -1)
    if fmt == "e4m3":
        vals = words.view(ml_dtypes.float8_e4m3fn).astype(np.float64)
    else:
        nib = np.empty((g, 128, n, 4), np.uint8)
        nib[..., 0::2] = words & 0xF
        nib[..., 1::2] = words >> 4
        vals = E2M1[nib]
    vals = vals * np.repeat(np.exp2(scales.astype(np.float64) - 127.0), 8, axis=1)[..., None]
    return vals.transpose(0, 1, 3, 2).reshape(g * 512, n)


K, L, Q, I = 512, 512, 512, 1024


def setup_inputs():
    n = np.random.standard_normal
    fk = mx_kscale(K)
    fl = mx_kscale(L)
    qap = pack_weight(n((K, Q)) * 0.03 * fk[:, None], "e4m3")
    qbp = pack_weight(n((L, Q)) * 0.03 * fl[:, None], "e2m1")
    kbp = pack_weight(n((L, I)) / fl[:, None], "e4m3")
    return {
        "qa_words": qap[0],
        "qa_scales": qap[1],
        "ka": (n((K, I)) / fk[:, None]).astype(np.float32),
        "qb_words": qbp[0],
        "qb_scales": qbp[1],
        "kb_words": kbp[0],
        "kb_scales": kbp[1],
        "cw1": (np.random.uniform(0.5, 2.0, (1, I))).astype(np.float32),
    }


def reference(qa_words, qa_scales, ka, qb_words, qb_scales, kb_words, kb_scales, cw1):
    qau = unpack_weight(qa_words, qa_scales, "e4m3")
    qbu = unpack_weight(qb_words, qb_scales, "e2m1")
    kbu = unpack_weight(kb_words, kb_scales, "e4m3")
    kaq = mxq(f64(ka), 0, "e4m3")
    a = qau.T @ kaq + qbu.T @ kbu
    e = np.exp(a)
    y = 256.0 * e * f64(cw1) / np.sum(e, axis=1, keepdims=True)
    return y

@@ -1,0 +1,306 @@
+from contextlib import ExitStack
+
+import concourse.mybir as mybir
+from concourse.masks import make_identity
+
+K, L, Q, I = 512, 512, 512, 1024
+FLOPS = 2 * (K + L) * Q * I
+
+F32 = mybir.dt.float32
+BF16 = mybir.dt.bfloat16
+I32 = mybir.dt.int32
+U32 = mybir.dt.uint32
+U8 = mybir.dt.uint8
+FP8X4 = mybir.dt.float8_e4m3fn_x4
+FP4X4 = mybir.dt.float4_e2m1fn_x4
+ALU = mybir.AluOpType
+ACT = mybir.ActivationFunctionType
+AX = mybir.AxisListType
+
+P = 128
+PACK = 4
+TILES = Q // P
+HALF = 512
+SPANS = [(0, 256), (256, 512), (512, 768), (768, 1024)]
+KB_SPANS = [(0, 512), (512, 768), (768, 1024)]
+EARLY = 2
+CHUNKS = len(SPANS)
+N_FP4 = 128
+RUN = 4
+SHARES = [(168, 88, 0), (0, 256, 0), (0, 256, 0), (0, 256, 0)]
+
+
+def tile_mix_shares_from_two_sources_kernel(
+    tc, qa_words, qa_scales, ka, qb_words, qb_scales, kb_words, kb_scales, cw1, out
+):
+    nc = tc.nc
+    with ExitStack() as ctx:
+        keep = ctx.enter_context(tc.tile_pool(name="keep", bufs=1))
+        psum = ctx.enter_context(tc.psum_pool(name="psum", bufs=1))
+        ctx.enter_context(tc.manual_schedule())
+
+        def sb(name, shape, dtype):
+            return keep.tile(shape, dtype, name=name, align_bytes=64)
+
+        qa_plane = sb("qa_plane", [P, Q], U8)
+        qb_plane = sb("qb_plane", [P, Q], U8)
+        kb_plane = sb("kb_plane", [P, I], U8)
+        qa_codes = sb("qa_codes", [P, Q], U32)
+        qb_codes = sb("qb_codes", [P, 2 * Q], U8)
+        widths = [b - a for a, b in SPANS]
+        kb_codes = [sb("kb_codes%d" % j, [P, b - a], U32) for j, (a, b) in enumerate(KB_SPANS)]
+        raw = [sb("raw%d" % c, [P, PACK, w], F32) for c, w in enumerate(widths)]
+        grouped = [sb("grouped%d" % c, [P, w * PACK], BF16) for c, w in enumerate(widths)]
+        ka_codes = [sb("ka_codes%d" % c, [P, w], U32) for c, w in enumerate(widths)]
+        ka_plane = [sb("ka_plane%d" % c, [P, w], U8) for c, w in enumerate(widths)]
+        cw_raw = sb("cw_raw", [P, 2 * PACK], F32)
+        cw_cols = sb("cw_cols", [P, 2 * PACK], F32)
+        ident = sb("ident", [P, P], F32)
+        warm_in = sb("warm_in", [P, 1], F32)
+        warm_out = sb("warm_out", [P, 1], F32)
+        neg_part = sb("neg_part", [P, TILES, CHUNKS], F32)
+        neg_first = sb("neg_first", [P, EARLY], F32)
+        neg_all = [sb("neg_all%d" % t, [P, 1], F32) for t in range(TILES)]
+        sums = [[sb("sum%d_%d" % (t, h), [P, 1], F32) for h in range(2)] for t in range(TILES)]
+        corr = [sb("corr%d" % t, [P, 1], F32) for t in range(TILES)]
+        den = [sb("den%d" % t, [P, 1], F32) for t in range(TILES)]
+        factor = [[sb("factor%d_%d" % (t, h), [P, 1], F32) for h in range(2)] for t in range(TILES)]
+        expo = [[sb("expo%d_%d" % (t, h), [P, HALF], F32) for h in range(2)] for t in range(TILES)]
+        res = [[sb("res%d_%d" % (t, h), [P, HALF], F32) for h in range(2)] for t in range(TILES)]
+        score = [
+            [psum.tile([P, HALF], F32, name="score%d_%d" % (t, h), tag="bank%d" % (2 * t + h)) for h in range(2)]
+            for t in range(TILES)
+        ]
+
+        def load_plane(engine, plane, scales, r):
+            engine.dma_start(out=plane[r:P:32, :].bitcast(I32), in_=scales[0, r:16:4, :].bitcast(I32))
+
+        def load_ka(c):
+            a, b = SPANS[c]
+            nc.sync.dma_start(out=raw[c][:], in_=ka[:, a:b].rearrange("(p j) w -> p j w", j=PACK))
+
+        kb_rows = kb_words[0].rearrange("p n t -> p (n t)")
+
+        def load_kb(j):
+            a, b = KB_SPANS[j]
+            nc.sync.dma_start(out=kb_codes[j][:].bitcast(I32), in_=kb_rows[:, 4 * a : 4 * b].bitcast(I32))
+
+        def kb_window(col, step):
+            for j, (a, b) in enumerate(KB_SPANS):
+                if a <= col < b:
+                    return kb_codes[j][:, col - a : col - a + step]
+
+        def cast(c, which):
+            lo = sum(SHARES[c][:which])
+            hi = lo + SHARES[c][which]
+            if hi == lo:
+                return
+            dst = grouped[c][:, PACK * lo : PACK * hi].rearrange("p (c i t) -> p c t i", i=RUN, t=PACK)
+            src = raw[c][:, :, lo:hi].rearrange("p t (c i) -> p c t i", i=RUN)
+            if which == 0:
+                nc.vector.tensor_copy(out=dst, in_=src)
+            elif which == 1:
+                nc.scalar.copy(out=dst, in_=src)
+            else:
+                nc.gpsimd.tensor_scalar(out=dst, in0=src, scalar1=1.0, scalar2=0.0, op0=ALU.mult, op1=ALU.add)
+
+        def quantize(c):
+            nc.vector.quantize_mx(out=ka_codes[c][:].bitcast(FP8X4), scales=ka_plane[c][:], in_=grouped[c][:])
+
+        def position_passes(c):
+            a, b = SPANS[c]
+            step = HALF if b - a == HALF else N_FP4
+            for t in range(TILES):
+                for col in range(a, b, step):
+                    nc.tensor.matmul_mx(
+                        out=score[t][col // HALF][:, col % HALF : col % HALF + step],
+                        lhsT=qb_codes[:, 2 * P * t : 2 * P * (t + 1)].bitcast(FP4X4),
+                        lhsT_scale=qb_plane[:, P * t : P * (t + 1)],
+                        rhs=kb_window(col, step).bitcast(FP8X4),
+                        rhs_scale=kb_plane[:, col : col + step],
+                        start=(col == a),
+                        stop=False,
+                    )
+
+        def content_passes(c):
+            a, b = SPANS[c]
+            for t in range(TILES):
+                nc.tensor.matmul_mx(
+                    out=score[t][a // HALF][:, a % HALF : a % HALF + b - a],
+                    lhsT=qa_codes[:, P * t : P * (t + 1)].bitcast(FP8X4),
+                    lhsT_scale=qa_plane[:, P * t : P * (t + 1)],
+                    rhs=ka_codes[c][:].bitcast(FP8X4),
+                    rhs_scale=ka_plane[c][:],
+                    start=False,
+                    stop=True,
+                )
+
+        def chunk_max(c, t):
+            a, b = SPANS[c]
+            nc.vector.tensor_reduce(
+                out=neg_part[:, t, c : c + 1],
+                in_=score[t][a // HALF][:, a % HALF : a % HALF + b - a],
+                axis=AX.X,
+                op=ALU.max,
+                negate=True,
+            )
+
+        def exponentials(t, h):
+            bias = neg_first[:, t : t + 1] if h == 0 and t < EARLY else neg_all[t][:]
+            nc.scalar.activation(
+                out=expo[t][h][:], in_=score[t][h][:], func=ACT.Exp, bias=bias, scale=1.0, accum_out=sums[t][h][:]
+            )
+
+        def row_max(t):
+            nc.vector.tensor_reduce(out=neg_all[t][:], in_=neg_part[:, t, :], axis=AX.X, op=ALU.min)
+
+        def correction(t):
+            nc.scalar.activation(
+                out=corr[t][:], in_=neg_first[:, t : t + 1], func=ACT.Exp, bias=neg_all[t][:], scale=-1.0
+            )
+
+        def denominator(t):
+            nc.scalar.activation(
+                out=den[t][:], in_=sums[t][0][:], func=ACT.Identity, bias=sums[t][1][:], scale=corr[t][:] if t < EARLY else 1.0
+            )
+
+        def load_qa():
+            nc.sync.dma_start(
+                out=qa_codes[:].bitcast(I32), in_=qa_words[0].rearrange("p n t -> p (n t)").bitcast(I32)
+            )
+
+        def load_qb():
+            nc.sync.dma_start(out=qb_codes[:].bitcast(I32), in_=qb_words[0].bitcast(I32))
+
+        def load_cw(engine):
+            engine.dma_start(
+                out=cw_raw[:].rearrange("p (h c) -> p h c", c=PACK),
+                in_=cw1[0].rearrange("(h p c) -> p h c", h=2, c=PACK),
+            )
+
+        weight = [None, None]
+
+        def spread(h, t):
+            weight[h] = psum.tile([P, HALF], F32, name="weight%d" % h, tag="bank%d" % (2 * t))
+            for c in range(PACK):
+                j = PACK * h + c
+                nc.tensor.transpose(weight[h][:, c:HALF:PACK], cw_cols[:, j : j + 1].to_broadcast([P, P]), ident[:])
+
+        def scale_cw():
+            nc.vector.tensor_scalar(out=cw_cols[:], in0=cw_raw[:], scalar1=256.0, scalar2=None, op0=ALU.mult)
+
+        def first_max():
+            nc.vector.tensor_reduce(out=neg_first[:], in_=neg_part[:, 0:EARLY, 0:2], axis=AX.X, op=ALU.min)
+
+        def reciprocal(t):
+            nc.vector.reciprocal(out=factor[t][1][:], in_=den[t][:])
+
+        def first_factor(t):
+            nc.vector.tensor_scalar(
+                out=factor[t][0][:], in0=factor[t][1][:], scalar1=corr[t][:], scalar2=None, op0=ALU.mult
+            )
+
+        def finish(t, h, lo=0, hi=HALF):
+            nc.vector.scalar_tensor_tensor(
+                out=res[t][h][:, lo:hi],
+                in0=expo[t][h][:, lo:hi],
+                scalar=factor[t][h if t < EARLY else 1][:],
+                in1=weight[h][:, lo:hi],
+                op0=ALU.mult,
+                op1=ALU.mult,
+            )
+            nc.sync.dma_start(out=out[P * t : P * (t + 1), HALF * h + lo : HALF * h + hi], in_=res[t][h][:, lo:hi])
+
+        def casts(c):
+            for which in range(3):
+                cast(c, which)
+
+        def passes(c):
+            position_passes(c)
+            content_passes(c)
+
+        plane_loads = [
+            (plane, scales, r)
+            for plane, scales in ((qa_plane, qa_scales), (qb_plane, qb_scales), (kb_plane, kb_scales))
+            for r in range(4)
+        ]
+
+        def load_planes(engine, lo, hi):
+            for plane, scales, r in plane_loads[lo:hi]:
+                load_plane(engine, plane, scales, r)
+
+        nc.vector.memset(qa_plane[:].bitcast(I32), 0)
+        nc.vector.memset(qb_plane[:].bitcast(I32), 0)
+        nc.vector.memset(kb_plane[:].bitcast(I32), 0)
+        nc.vector.memset(warm_in[:], 0.0)
+        nc.scalar.activation(out=warm_out[:], in_=warm_in[:], func=ACT.Exp)
+        load_qa()
+        load_qb()
+        load_planes(nc.sync, 0, 5)
+        load_ka(0)
+        load_kb(0)
+        load_planes(nc.sync, 5, 10)
+        load_planes(nc.gpsimd, 10, 12)
+        load_cw(nc.gpsimd)
+        make_identity(nc, ident[:])
+        load_ka(1)
+        load_kb(1)
+        load_ka(2)
+        load_ka(3)
+        load_kb(2)
+
+        for c in range(2):
+            casts(c)
+            quantize(c)
+            passes(c)
+            for t in range(TILES):
+                chunk_max(c, t)
+        casts(2)
+        scale_cw()
+        first_max()
+        quantize(2)
+        passes(2)
+        for t in range(TILES):
+            chunk_max(2, t)
+        exponentials(0, 0)
+        spread(1, 0)
+        casts(3)
+        exponentials(1, 0)
+        quantize(3)
+        passes(3)
+        spread(0, 1)
+        chunk_max(3, 0)
+        chunk_max(3, 1)
+        row_max(0)
+        correction(0)
+        exponentials(0, 1)
+        chunk_max(3, 2)
+        row_max(1)
+        correction(1)
+        denominator(0)
+        exponentials(1, 1)
+        chunk_max(3, 3)
+        row_max(2)
+        reciprocal(0)
+        row_max(3)
+        denominator(1)
+        exponentials(2, 1)
+        exponentials(2, 0)
+        denominator(2)
+        exponentials(3, 1)
+        exponentials(3, 0)
+        denominator(3)
+        first_factor(0)
+        finish(0, 1)
+        reciprocal(1)
+        finish(0, 0)
+        first_factor(1)
+        finish(1, 1)
+        reciprocal(2)
+        finish(1, 0)
+        finish(2, 1)
+        reciprocal(3)
+        finish(2, 0)
+        finish(3, 1)
+        finish(3, 0, 0, 256)
+        finish(3, 0, 256, 512)

@@ -22,8 +22,8 @@ PACK = 4
 TILES = Q // P
 HALF = 512
 SPANS = [(0, 256), (256, 512), (512, 768), (768, 1024)]
-KB_SPANS = [(0, 512), (512, 768), (768, 1024)]
-EARLY = 2
+KB_SPANS = [(0, 512), (512, 1024)]
+EARLY = 3
 CHUNKS = len(SPANS)
 N_FP4 = 128
 RUN = 4
@@ -55,6 +55,8 @@ def tile_mix_shares_from_two_sources_kernel(
         ka_plane = [sb("ka_plane%d" % c, [P, w], U8) for c, w in enumerate(widths)]
         cw_raw = sb("cw_raw", [P, 2 * PACK], F32)
         cw_cols = sb("cw_cols", [P, 2 * PACK], F32)
+        cw_first = sb("cw_first", [P, HALF], F32)
+        weighted = [sb("weighted%d" % t, [P, HALF], F32) for t in range(TILES)]
         ident = sb("ident", [P, P], F32)
         warm_in = sb("warm_in", [P, 1], F32)
         warm_out = sb("warm_out", [P, 1], F32)
@@ -107,10 +109,10 @@ def tile_mix_shares_from_two_sources_kernel(
         def quantize(c):
             nc.vector.quantize_mx(out=ka_codes[c][:].bitcast(FP8X4), scales=ka_plane[c][:], in_=grouped[c][:])
 
-        def position_passes(c):
+        def position_passes(c, tiles=range(TILES)):
             a, b = SPANS[c]
             step = HALF if b - a == HALF else N_FP4
-            for t in range(TILES):
+            for t in tiles:
                 for col in range(a, b, step):
                     nc.tensor.matmul_mx(
                         out=score[t][col // HALF][:, col % HALF : col % HALF + step],
@@ -122,9 +124,9 @@ def tile_mix_shares_from_two_sources_kernel(
                         stop=False,
                     )
 
-        def content_passes(c):
+        def content_passes(c, tiles=range(TILES)):
             a, b = SPANS[c]
-            for t in range(TILES):
+            for t in tiles:
                 nc.tensor.matmul_mx(
                     out=score[t][a // HALF][:, a % HALF : a % HALF + b - a],
                     lhsT=qa_codes[:, P * t : P * (t + 1)].bitcast(FP8X4),
@@ -187,10 +189,10 @@ def tile_mix_shares_from_two_sources_kernel(
                 nc.tensor.transpose(weight[h][:, c:HALF:PACK], cw_cols[:, j : j + 1].to_broadcast([P, P]), ident[:])
 
         def scale_cw():
-            nc.vector.tensor_scalar(out=cw_cols[:], in0=cw_raw[:], scalar1=256.0, scalar2=None, op0=ALU.mult)
+            nc.gpsimd.tensor_scalar(out=cw_cols[:], in0=cw_raw[:], scalar1=256.0, scalar2=0.0, op0=ALU.mult, op1=ALU.add)
 
-        def first_max():
-            nc.vector.tensor_reduce(out=neg_first[:], in_=neg_part[:, 0:EARLY, 0:2], axis=AX.X, op=ALU.min)
+        def first_max(lo, hi):
+            nc.vector.tensor_reduce(out=neg_first[:, lo:hi], in_=neg_part[:, lo:hi, 0:2], axis=AX.X, op=ALU.min)
 
         def reciprocal(t):
             nc.vector.reciprocal(out=factor[t][1][:], in_=den[t][:])
@@ -211,6 +213,23 @@ def tile_mix_shares_from_two_sources_kernel(
             )
             nc.sync.dma_start(out=out[P * t : P * (t + 1), HALF * h + lo : HALF * h + hi], in_=res[t][h][:, lo:hi])
 
+        def load_cw_first():
+            nc.sync.dma_start(out=cw_first[:], in_=cw1[0, 0:HALF].partition_broadcast(P))
+
+        def premultiply(t):
+            nc.gpsimd.tensor_tensor(out=weighted[t][:], in0=expo[t][0][:], in1=cw_first[:], op=ALU.mult)
+
+        def first_factor_scaled(t):
+            nc.vector.tensor_scalar(
+                out=factor[t][0][:], in0=factor[t][1][:], scalar1=corr[t][:], scalar2=256.0, op0=ALU.mult, op1=ALU.mult
+            )
+
+        def finish_weighted(t, lo=0, hi=HALF):
+            nc.scalar.activation(
+                out=res[t][0][:, lo:hi], in_=weighted[t][:, lo:hi], func=ACT.Copy, scale=factor[t][0][:]
+            )
+            nc.sync.dma_start(out=out[P * t : P * (t + 1), lo:hi], in_=res[t][0][:, lo:hi])
+
         def casts(c):
             for which in range(3):
                 cast(c, which)
@@ -221,7 +240,7 @@ def tile_mix_shares_from_two_sources_kernel(
 
         plane_loads = [
             (plane, scales, r)
-            for plane, scales in ((qa_plane, qa_scales), (qb_plane, qb_scales), (kb_plane, kb_scales))
+            for plane, scales in ((qb_plane, qb_scales), (kb_plane, kb_scales), (qa_plane, qa_scales))
             for r in range(4)
         ]
 
@@ -229,51 +248,69 @@ def tile_mix_shares_from_two_sources_kernel(
             for plane, scales, r in plane_loads[lo:hi]:
                 load_plane(engine, plane, scales, r)
 
-        nc.vector.memset(qa_plane[:].bitcast(I32), 0)
         nc.vector.memset(qb_plane[:].bitcast(I32), 0)
         nc.vector.memset(kb_plane[:].bitcast(I32), 0)
         nc.vector.memset(warm_in[:], 0.0)
+        nc.gpsimd.memset(qa_plane[:].bitcast(I32), 0)
         nc.scalar.activation(out=warm_out[:], in_=warm_in[:], func=ACT.Exp)
         load_qa()
-        load_qb()
         load_planes(nc.sync, 0, 5)
+        load_qb()
         load_ka(0)
         load_kb(0)
         load_planes(nc.sync, 5, 10)
         load_planes(nc.gpsimd, 10, 12)
         load_cw(nc.gpsimd)
         make_identity(nc, ident[:])
-        load_ka(1)
-        load_kb(1)
-        load_ka(2)
-        load_ka(3)
-        load_kb(2)
-
-        for c in range(2):
-            casts(c)
-            quantize(c)
-            passes(c)
-            for t in range(TILES):
-                chunk_max(c, t)
-        casts(2)
         scale_cw()
-        first_max()
+        load_ka(1)
+        load_ka(2)
+        load_kb(1)
+        load_ka(3)
+
+        def both(c, t):
+            position_passes(c, [t])
+            content_passes(c, [t])
+
+        casts(0)
+        quantize(0)
+        position_passes(0)
+        content_passes(0)
+        casts(1)
+        chunk_max(0, 0)
+        quantize(1)
+        casts(2)
+        both(1, 0)
+        for t in range(1, TILES):
+            chunk_max(0, t)
+            both(1, t)
+        chunk_max(1, 0)
         quantize(2)
-        passes(2)
-        for t in range(TILES):
-            chunk_max(2, t)
-        exponentials(0, 0)
-        spread(1, 0)
         casts(3)
-        exponentials(1, 0)
+        for t in range(TILES):
+            both(2, t)
+        chunk_max(1, 1)
+        chunk_max(1, 2)
+        chunk_max(1, 3)
+        first_max(0, EARLY)
+        chunk_max(2, 0)
+        for t in range(EARLY):
+            exponentials(t, 0)
         quantize(3)
-        passes(3)
-        spread(0, 1)
+        both(3, 0)
+        chunk_max(2, 1)
+        both(3, 1)
+        chunk_max(2, 2)
+        both(3, 2)
         chunk_max(3, 0)
-        chunk_max(3, 1)
+        chunk_max(2, 3)
+        both(3, 3)
+        spread(1, 0)
+        spread(0, 1)
         row_max(0)
         correction(0)
         exponentials(0, 1)
+        chunk_max(3, 1)
         chunk_max(3, 2)
         row_max(1)
         correction(1)
@@ -283,14 +320,14 @@ def tile_mix_shares_from_two_sources_kernel(
         row_max(2)
         reciprocal(0)
         row_max(3)
+        first_factor(0)
+        correction(2)
         denominator(1)
         exponentials(2, 1)
-        exponentials(2, 0)
+        exponentials(3, 0)
         denominator(2)
         exponentials(3, 1)
-        exponentials(3, 0)
         denominator(3)
-        first_factor(0)
         finish(0, 1)
         reciprocal(1)
         finish(0, 0)
@@ -298,6 +335,7 @@ def tile_mix_shares_from_two_sources_kernel(
         finish(1, 1)
         reciprocal(2)
         finish(1, 0)
+        first_factor(2)
         finish(2, 1)
         reciprocal(3)
         finish(2, 0)

@@ -27,7 +27,7 @@ EARLY = 3
 CHUNKS = len(SPANS)
 N_FP4 = 128
 RUN = 4
-SHARES = [(168, 88, 0), (0, 256, 0), (0, 256, 0), (0, 256, 0)]
+SHARES = [(168, 88, 0), (128, 128, 0), (128, 128, 0), (160, 96, 0)]
 
 
 def tile_mix_shares_from_two_sources_kernel(
@@ -57,11 +57,12 @@ def tile_mix_shares_from_two_sources_kernel(
         cw_cols = sb("cw_cols", [P, 2 * PACK], F32)
         cw_first = sb("cw_first", [P, HALF], F32)
         weighted = [sb("weighted%d" % t, [P, HALF], F32) for t in range(TILES)]
+        negated = [sb("negated%d" % t, [P, HALF], F32) for t in range(TILES)]
         ident = sb("ident", [P, P], F32)
         warm_in = sb("warm_in", [P, 1], F32)
         warm_out = sb("warm_out", [P, 1], F32)
         neg_part = sb("neg_part", [P, TILES, CHUNKS], F32)
-        neg_first = sb("neg_first", [P, EARLY], F32)
+        neg_first = sb("neg_first", [P, TILES], F32)
         neg_all = [sb("neg_all%d" % t, [P, 1], F32) for t in range(TILES)]
         sums = [[sb("sum%d_%d" % (t, h), [P, 1], F32) for h in range(2)] for t in range(TILES)]
         corr = [sb("corr%d" % t, [P, 1], F32) for t in range(TILES)]
@@ -124,6 +125,28 @@ def tile_mix_shares_from_two_sources_kernel(
                         stop=False,
                     )
 
+        def wide_position_pass(t):
+            nc.tensor.matmul_mx(
+                out=score[t][1][:],
+                lhsT=qb_codes[:, 2 * P * t : 2 * P * (t + 1)].bitcast(FP4X4),
+                lhsT_scale=qb_plane[:, P * t : P * (t + 1)],
+                rhs=kb_window(HALF, HALF).bitcast(FP8X4),
+                rhs_scale=kb_plane[:, HALF:I],
+                start=True,
+                stop=False,
+            )
+
+        def second_max(t):
+            nc.vector.tensor_scalar(
+                out=negated[t][:],
+                in0=score[t][1][:],
+                scalar1=-1.0,
+                scalar2=neg_first[:, t : t + 1],
+                op0=ALU.mult,
+                op1=ALU.min,
+                accum_out=neg_all[t][:],
+            )
+
         def content_passes(c, tiles=range(TILES)):
             a, b = SPANS[c]
             for t in tiles:
@@ -134,7 +157,7 @@ def tile_mix_shares_from_two_sources_kernel(
                     rhs=ka_codes[c][:].bitcast(FP8X4),
                     rhs_scale=ka_plane[c][:],
                     start=False,
-                    stop=True,
+                    stop=(c != 2),
                 )
 
         def chunk_max(c, t):
@@ -150,7 +173,12 @@ def tile_mix_shares_from_two_sources_kernel(
         def exponentials(t, h):
             bias = neg_first[:, t : t + 1] if h == 0 and t < EARLY else neg_all[t][:]
             nc.scalar.activation(
-                out=expo[t][h][:], in_=score[t][h][:], func=ACT.Exp, bias=bias, scale=1.0, accum_out=sums[t][h][:]
+                out=expo[t][h][:],
+                in_=negated[t][:] if h else score[t][h][:],
+                func=ACT.Exp,
+                bias=bias,
+                scale=-1.0 if h else 1.0,
+                accum_out=sums[t][h][:],
             )
 
         def row_max(t):
@@ -250,9 +278,7 @@ def tile_mix_shares_from_two_sources_kernel(
 
         nc.vector.memset(qb_plane[:].bitcast(I32), 0)
         nc.vector.memset(kb_plane[:].bitcast(I32), 0)
-        nc.vector.memset(warm_in[:], 0.0)
         nc.gpsimd.memset(qa_plane[:].bitcast(I32), 0)
-        nc.scalar.activation(out=warm_out[:], in_=warm_in[:], func=ACT.Exp)
         load_qa()
         load_planes(nc.sync, 0, 5)
         load_qb()
@@ -265,8 +291,8 @@ def tile_mix_shares_from_two_sources_kernel(
         scale_cw()
         load_ka(1)
         load_ka(2)
-        load_kb(1)
         load_ka(3)
+        load_kb(1)
 
         def both(c, t):
             position_passes(c, [t])
@@ -274,52 +300,46 @@ def tile_mix_shares_from_two_sources_kernel(
 
         casts(0)
         quantize(0)
-        position_passes(0)
-        content_passes(0)
-        casts(1)
+        for t in range(TILES):
+            both(0, t)
         chunk_max(0, 0)
+        casts(1)
+        chunk_max(0, 1)
         quantize(1)
-        casts(2)
-        both(1, 0)
-        for t in range(1, TILES):
-            chunk_max(0, t)
+        chunk_max(0, 2)
+        chunk_max(0, 3)
+        for t in range(TILES):
             both(1, t)
+        casts(2)
         chunk_max(1, 0)
         quantize(2)
-        casts(3)
-        for t in range(TILES):
-            both(2, t)
         chunk_max(1, 1)
-        chunk_max(1, 2)
-        chunk_max(1, 3)
-        first_max(0, EARLY)
-        chunk_max(2, 0)
-        for t in range(EARLY):
-            exponentials(t, 0)
+        casts(3)
+        first_max(0, 2)
         quantize(3)
-        both(3, 0)
-        chunk_max(2, 1)
-        both(3, 1)
-        chunk_max(2, 2)
-        both(3, 2)
-        chunk_max(3, 0)
-        chunk_max(2, 3)
-        both(3, 3)
+        for t in range(TILES):
+            wide_position_pass(t)
+            content_passes(2, [t])
+            content_passes(3, [t])
+        exponentials(0, 0)
+        exponentials(1, 0)
         spread(1, 0)
         spread(0, 1)
-        row_max(0)
+        chunk_max(1, 2)
+        chunk_max(1, 3)
+        first_max(2, 3)
+        exponentials(2, 0)
+        second_max(0)
+        first_max(3, TILES)
         correction(0)
         exponentials(0, 1)
-        chunk_max(3, 1)
-        chunk_max(3, 2)
-        row_max(1)
+        second_max(1)
         correction(1)
         denominator(0)
         exponentials(1, 1)
-        chunk_max(3, 3)
-        row_max(2)
+        second_max(2)
         reciprocal(0)
-        row_max(3)
+        second_max(3)
         first_factor(0)
         correction(2)
         denominator(1)

@@ -19,15 +19,19 @@ AX = mybir.AxisListType
 
 P = 128
 PACK = 4
+SCALE_ROWS = 16
+QUADRANT = 32
 TILES = Q // P
-HALF = 512
-SPANS = [(0, 256), (256, 512), (512, 768), (768, 1024)]
-KB_SPANS = [(0, 512), (512, 1024)]
-EARLY = 3
-CHUNKS = len(SPANS)
-N_FP4 = 128
-RUN = 4
-SHARES = [(168, 88, 0), (128, 128, 0), (128, 128, 0), (160, 96, 0)]
+HALF = I // 2
+CHUNK = 256
+CHUNKS = I // CHUNK
+NARROW = 128
+PIECE = HALF // 2
+OUT_SCALE = 256.0
+VECTOR_COLUMNS = (168, 128, 128, 160)
+SECOND_BANK = (4, 5, 0, 1)
+WEIGHT_BANK = (6, 7)
+SCALE_LOADS_PER_ROUND = 5
 
 
 def tile_mix_shares_from_two_sources_kernel(
@@ -42,101 +46,129 @@ def tile_mix_shares_from_two_sources_kernel(
         def sb(name, shape, dtype):
             return keep.tile(shape, dtype, name=name, align_bytes=64)
 
+        def per_tile(name, width):
+            return [sb("%s%d" % (name, t), [P, width], F32) for t in range(TILES)]
+
+        def per_half(name, width):
+            return [[sb("%s%d_%d" % (name, t, h), [P, width], F32) for h in range(2)] for t in range(TILES)]
+
         qa_plane = sb("qa_plane", [P, Q], U8)
         qb_plane = sb("qb_plane", [P, Q], U8)
         kb_plane = sb("kb_plane", [P, I], U8)
         qa_codes = sb("qa_codes", [P, Q], U32)
         qb_codes = sb("qb_codes", [P, 2 * Q], U8)
-        widths = [b - a for a, b in SPANS]
-        kb_codes = [sb("kb_codes%d" % j, [P, b - a], U32) for j, (a, b) in enumerate(KB_SPANS)]
-        raw = [sb("raw%d" % c, [P, PACK, w], F32) for c, w in enumerate(widths)]
-        grouped = [sb("grouped%d" % c, [P, w * PACK], BF16) for c, w in enumerate(widths)]
-        ka_codes = [sb("ka_codes%d" % c, [P, w], U32) for c, w in enumerate(widths)]
-        ka_plane = [sb("ka_plane%d" % c, [P, w], U8) for c, w in enumerate(widths)]
+        kb_codes = [sb("kb_codes%d" % h, [P, HALF], U32) for h in range(2)]
+        raw = [sb("raw%d" % c, [P, PACK, CHUNK], F32) for c in range(CHUNKS)]
+        grouped = [sb("grouped%d" % c, [P, CHUNK * PACK], BF16) for c in range(CHUNKS)]
+        ka_codes = [sb("ka_codes%d" % c, [P, CHUNK], U32) for c in range(CHUNKS)]
+        ka_plane = [sb("ka_plane%d" % c, [P, CHUNK], U8) for c in range(CHUNKS)]
         cw_raw = sb("cw_raw", [P, 2 * PACK], F32)
         cw_cols = sb("cw_cols", [P, 2 * PACK], F32)
-        cw_first = sb("cw_first", [P, HALF], F32)
-        weighted = [sb("weighted%d" % t, [P, HALF], F32) for t in range(TILES)]
-        negated = [sb("negated%d" % t, [P, HALF], F32) for t in range(TILES)]
+        first_weight = sb("first_weight", [P, HALF], F32)
         ident = sb("ident", [P, P], F32)
-        warm_in = sb("warm_in", [P, 1], F32)
-        warm_out = sb("warm_out", [P, 1], F32)
-        neg_part = sb("neg_part", [P, TILES, CHUNKS], F32)
+        neg_chunk = sb("neg_chunk", [P, TILES, 2], F32)
         neg_first = sb("neg_first", [P, TILES], F32)
-        neg_all = [sb("neg_all%d" % t, [P, 1], F32) for t in range(TILES)]
-        sums = [[sb("sum%d_%d" % (t, h), [P, 1], F32) for h in range(2)] for t in range(TILES)]
-        corr = [sb("corr%d" % t, [P, 1], F32) for t in range(TILES)]
-        den = [sb("den%d" % t, [P, 1], F32) for t in range(TILES)]
-        factor = [[sb("factor%d_%d" % (t, h), [P, 1], F32) for h in range(2)] for t in range(TILES)]
-        expo = [[sb("expo%d_%d" % (t, h), [P, HALF], F32) for h in range(2)] for t in range(TILES)]
-        res = [[sb("res%d_%d" % (t, h), [P, HALF], F32) for h in range(2)] for t in range(TILES)]
-        score = [
-            [psum.tile([P, HALF], F32, name="score%d_%d" % (t, h), tag="bank%d" % (2 * t + h)) for h in range(2)]
-            for t in range(TILES)
+        neg_row = per_tile("neg_row", 1)
+        negated = per_tile("negated", HALF)
+        sums = per_half("sum", 1)
+        corr = per_tile("corr", 1)
+        den = per_tile("den", 1)
+        factor = per_half("factor", 1)
+        expo = per_half("expo", HALF)
+        res = per_half("res", HALF)
+        weighted = {t: sb("weighted%d" % t, [P, HALF], F32) for t in (0, 1, 3)}
+        score = [[psum.tile([P, HALF], F32, name="score%d_0" % t, tag="bank%d" % t), None] for t in range(TILES)]
+        weight = [psum.tile([P, PACK, P], F32, name="weight%d" % h, tag="bank%d" % WEIGHT_BANK[h]) for h in range(2)]
+
+        scale_loads = [
+            (plane, scales, r)
+            for plane, scales in ((qb_plane, qb_scales), (kb_plane, kb_scales), (qa_plane, qa_scales))
+            for r in range(PACK)
         ]
 
-        def load_plane(engine, plane, scales, r):
-            engine.dma_start(out=plane[r:P:32, :].bitcast(I32), in_=scales[0, r:16:4, :].bitcast(I32))
+        def load_scales(engine, loads):
+            for plane, scales, r in loads:
+                engine.dma_start(
+                    out=plane[r:P:QUADRANT, :].bitcast(I32), in_=scales[0, r:SCALE_ROWS:PACK, :].bitcast(I32)
+                )
 
         def load_ka(c):
-            a, b = SPANS[c]
-            nc.sync.dma_start(out=raw[c][:], in_=ka[:, a:b].rearrange("(p j) w -> p j w", j=PACK))
+            columns = ka[:, c * CHUNK : (c + 1) * CHUNK]
+            nc.sync.dma_start(out=raw[c][:], in_=columns.rearrange("(p j) w -> p j w", j=PACK))
 
-        kb_rows = kb_words[0].rearrange("p n t -> p (n t)")
+        def load_kb(h):
+            rows = kb_words[0].rearrange("p n t -> p (n t)")
+            nc.sync.dma_start(
+                out=kb_codes[h][:].bitcast(I32), in_=rows[:, PACK * HALF * h : PACK * HALF * (h + 1)].bitcast(I32)
+            )
 
-        def load_kb(j):
-            a, b = KB_SPANS[j]
-            nc.sync.dma_start(out=kb_codes[j][:].bitcast(I32), in_=kb_rows[:, 4 * a : 4 * b].bitcast(I32))
-
-        def kb_window(col, step):
-            for j, (a, b) in enumerate(KB_SPANS):
-                if a <= col < b:
-                    return kb_codes[j][:, col - a : col - a + step]
-
-        def cast(c, which):
-            lo = sum(SHARES[c][:which])
-            hi = lo + SHARES[c][which]
-            if hi == lo:
-                return
-            dst = grouped[c][:, PACK * lo : PACK * hi].rearrange("p (c i t) -> p c t i", i=RUN, t=PACK)
-            src = raw[c][:, :, lo:hi].rearrange("p t (c i) -> p c t i", i=RUN)
-            if which == 0:
-                nc.vector.tensor_copy(out=dst, in_=src)
-            elif which == 1:
-                nc.scalar.copy(out=dst, in_=src)
-            else:
-                nc.gpsimd.tensor_scalar(out=dst, in0=src, scalar1=1.0, scalar2=0.0, op0=ALU.mult, op1=ALU.add)
+        def round_chunk(c):
+            split = VECTOR_COLUMNS[c]
+            dst = grouped[c][:].rearrange("p (w t) -> p w t", t=PACK)
+            src = raw[c][:].rearrange("p t w -> p w t")
+            nc.vector.tensor_copy(out=dst[:, :split, :], in_=src[:, :split, :])
+            nc.scalar.copy(out=dst[:, split:, :], in_=src[:, split:, :])
 
         def quantize(c):
             nc.vector.quantize_mx(out=ka_codes[c][:].bitcast(FP8X4), scales=ka_plane[c][:], in_=grouped[c][:])
 
-        def position_passes(c, tiles=range(TILES)):
-            a, b = SPANS[c]
-            step = HALF if b - a == HALF else N_FP4
-            for t in tiles:
-                for col in range(a, b, step):
-                    nc.tensor.matmul_mx(
-                        out=score[t][col // HALF][:, col % HALF : col % HALF + step],
-                        lhsT=qb_codes[:, 2 * P * t : 2 * P * (t + 1)].bitcast(FP4X4),
-                        lhsT_scale=qb_plane[:, P * t : P * (t + 1)],
-                        rhs=kb_window(col, step).bitcast(FP8X4),
-                        rhs_scale=kb_plane[:, col : col + step],
-                        start=(col == a),
-                        stop=False,
-                    )
-
-        def wide_position_pass(t):
+        def position_pass(t, col, width, start):
+            h, lo = divmod(col, HALF)
             nc.tensor.matmul_mx(
-                out=score[t][1][:],
+                out=score[t][h][:, lo : lo + width],
                 lhsT=qb_codes[:, 2 * P * t : 2 * P * (t + 1)].bitcast(FP4X4),
                 lhsT_scale=qb_plane[:, P * t : P * (t + 1)],
-                rhs=kb_window(HALF, HALF).bitcast(FP8X4),
-                rhs_scale=kb_plane[:, HALF:I],
-                start=True,
+                rhs=kb_codes[h][:, lo : lo + width].bitcast(FP8X4),
+                rhs_scale=kb_plane[:, col : col + width],
+                start=start,
                 stop=False,
             )
 
-        def second_max(t):
+        def content_pass(t, c, stop):
+            h, lo = divmod(c * CHUNK, HALF)
+            nc.tensor.matmul_mx(
+                out=score[t][h][:, lo : lo + CHUNK],
+                lhsT=qa_codes[:, P * t : P * (t + 1)].bitcast(FP8X4),
+                lhsT_scale=qa_plane[:, P * t : P * (t + 1)],
+                rhs=ka_codes[c][:].bitcast(FP8X4),
+                rhs_scale=ka_plane[c][:],
+                start=False,
+                stop=stop,
+            )
+
+        def chunk_scores(c):
+            for t in range(TILES):
+                for col in range(c * CHUNK, (c + 1) * CHUNK, NARROW):
+                    position_pass(t, col, NARROW, start=(col == c * CHUNK))
+                content_pass(t, c, stop=True)
+
+        def second_scores(t):
+            score[t][1] = psum.tile([P, HALF], F32, name="score%d_1" % t, tag="bank%d" % SECOND_BANK[t])
+            position_pass(t, HALF, HALF, start=True)
+            content_pass(t, 2, stop=False)
+            content_pass(t, 3, stop=True)
+
+        def spread_weights(h):
+            for j in range(PACK):
+                column = cw_cols[:, PACK * h + j : PACK * h + j + 1]
+                nc.tensor.transpose(weight[h][:, j, :], column.to_broadcast([P, P]), ident[:])
+
+        def by_word(ap):
+            return ap.rearrange("p (n j) -> p n j", j=PACK)
+
+        def chunk_max(c, t):
+            nc.vector.tensor_reduce(
+                out=neg_chunk[:, t, c : c + 1],
+                in_=score[t][0][:, c * CHUNK : (c + 1) * CHUNK],
+                axis=AX.X,
+                op=ALU.max,
+                negate=True,
+            )
+
+        def first_max(t):
+            nc.vector.tensor_reduce(out=neg_first[:, t : t + 1], in_=neg_chunk[:, t : t + 1, :], axis=AX.X, op=ALU.min)
+
+        def row_max(t):
             nc.vector.tensor_scalar(
                 out=negated[t][:],
                 in0=score[t][1][:],
@@ -144,85 +176,40 @@ def tile_mix_shares_from_two_sources_kernel(
                 scalar2=neg_first[:, t : t + 1],
                 op0=ALU.mult,
                 op1=ALU.min,
-                accum_out=neg_all[t][:],
+                accum_out=neg_row[t][:],
             )
 
-        def content_passes(c, tiles=range(TILES)):
-            a, b = SPANS[c]
-            for t in tiles:
-                nc.tensor.matmul_mx(
-                    out=score[t][a // HALF][:, a % HALF : a % HALF + b - a],
-                    lhsT=qa_codes[:, P * t : P * (t + 1)].bitcast(FP8X4),
-                    lhsT_scale=qa_plane[:, P * t : P * (t + 1)],
-                    rhs=ka_codes[c][:].bitcast(FP8X4),
-                    rhs_scale=ka_plane[c][:],
-                    start=False,
-                    stop=(c != 2),
-                )
-
-        def chunk_max(c, t):
-            a, b = SPANS[c]
-            nc.vector.tensor_reduce(
-                out=neg_part[:, t, c : c + 1],
-                in_=score[t][a // HALF][:, a % HALF : a % HALF + b - a],
-                axis=AX.X,
-                op=ALU.max,
-                negate=True,
-            )
-
-        def exponentials(t, h):
-            bias = neg_first[:, t : t + 1] if h == 0 and t < EARLY else neg_all[t][:]
+        def first_exp(t):
             nc.scalar.activation(
-                out=expo[t][h][:],
-                in_=negated[t][:] if h else score[t][h][:],
+                out=expo[t][0][:],
+                in_=score[t][0][:],
                 func=ACT.Exp,
-                bias=bias,
-                scale=-1.0 if h else 1.0,
-                accum_out=sums[t][h][:],
+                bias=neg_first[:, t : t + 1],
+                scale=1.0,
+                accum_out=sums[t][0][:],
             )
 
-        def row_max(t):
-            nc.vector.tensor_reduce(out=neg_all[t][:], in_=neg_part[:, t, :], axis=AX.X, op=ALU.min)
+        def second_exp(t):
+            nc.scalar.activation(
+                out=expo[t][1][:],
+                in_=negated[t][:],
+                func=ACT.Exp,
+                bias=neg_row[t][:],
+                scale=-1.0,
+                accum_out=sums[t][1][:],
+            )
 
         def correction(t):
             nc.scalar.activation(
-                out=corr[t][:], in_=neg_first[:, t : t + 1], func=ACT.Exp, bias=neg_all[t][:], scale=-1.0
+                out=corr[t][:], in_=neg_first[:, t : t + 1], func=ACT.Exp, bias=neg_row[t][:], scale=-1.0
             )
 
         def denominator(t):
             nc.scalar.activation(
-                out=den[t][:], in_=sums[t][0][:], func=ACT.Identity, bias=sums[t][1][:], scale=corr[t][:] if t < EARLY else 1.0
+                out=den[t][:], in_=sums[t][0][:], func=ACT.Identity, bias=sums[t][1][:], scale=corr[t][:]
             )
 
-        def load_qa():
-            nc.sync.dma_start(
-                out=qa_codes[:].bitcast(I32), in_=qa_words[0].rearrange("p n t -> p (n t)").bitcast(I32)
-            )
-
-        def load_qb():
-            nc.sync.dma_start(out=qb_codes[:].bitcast(I32), in_=qb_words[0].bitcast(I32))
-
-        def load_cw(engine):
-            engine.dma_start(
-                out=cw_raw[:].rearrange("p (h c) -> p h c", c=PACK),
-                in_=cw1[0].rearrange("(h p c) -> p h c", h=2, c=PACK),
-            )
-
-        weight = [None, None]
-
-        def spread(h, t):
-            weight[h] = psum.tile([P, HALF], F32, name="weight%d" % h, tag="bank%d" % (2 * t))
-            for c in range(PACK):
-                j = PACK * h + c
-                nc.tensor.transpose(weight[h][:, c:HALF:PACK], cw_cols[:, j : j + 1].to_broadcast([P, P]), ident[:])
-
-        def scale_cw():
-            nc.gpsimd.tensor_scalar(out=cw_cols[:], in0=cw_raw[:], scalar1=256.0, scalar2=0.0, op0=ALU.mult, op1=ALU.add)
-
-        def first_max(lo, hi):
-            nc.vector.tensor_reduce(out=neg_first[:, lo:hi], in_=neg_part[:, lo:hi, 0:2], axis=AX.X, op=ALU.min)
-
-        def reciprocal(t):
+        def second_factor(t):
             nc.vector.reciprocal(out=factor[t][1][:], in_=den[t][:])
 
         def first_factor(t):
@@ -230,135 +217,126 @@ def tile_mix_shares_from_two_sources_kernel(
                 out=factor[t][0][:], in0=factor[t][1][:], scalar1=corr[t][:], scalar2=None, op0=ALU.mult
             )
 
+        def store(t, h, lo, hi):
+            nc.sync.dma_start(out=out[P * t : P * (t + 1), HALF * h + lo : HALF * h + hi], in_=res[t][h][:, lo:hi])
+
         def finish(t, h, lo=0, hi=HALF):
             nc.vector.scalar_tensor_tensor(
-                out=res[t][h][:, lo:hi],
-                in0=expo[t][h][:, lo:hi],
-                scalar=factor[t][h if t < EARLY else 1][:],
-                in1=weight[h][:, lo:hi],
+                out=by_word(res[t][h][:, lo:hi]),
+                in0=by_word(expo[t][h][:, lo:hi]),
+                scalar=factor[t][h][:],
+                in1=weight[h][:, :, lo // PACK : hi // PACK].rearrange("p j n -> p n j"),
                 op0=ALU.mult,
                 op1=ALU.mult,
             )
-            nc.sync.dma_start(out=out[P * t : P * (t + 1), HALF * h + lo : HALF * h + hi], in_=res[t][h][:, lo:hi])
+            store(t, h, lo, hi)
 
-        def load_cw_first():
-            nc.sync.dma_start(out=cw_first[:], in_=cw1[0, 0:HALF].partition_broadcast(P))
+        def weigh_first(t):
+            nc.gpsimd.tensor_tensor(out=weighted[t][:], in0=expo[t][0][:], in1=first_weight[:], op=ALU.mult)
 
-        def premultiply(t):
-            nc.gpsimd.tensor_tensor(out=weighted[t][:], in0=expo[t][0][:], in1=cw_first[:], op=ALU.mult)
-
-        def first_factor_scaled(t):
-            nc.vector.tensor_scalar(
-                out=factor[t][0][:], in0=factor[t][1][:], scalar1=corr[t][:], scalar2=256.0, op0=ALU.mult, op1=ALU.mult
+        def finish_on_gpsimd(t):
+            nc.gpsimd.tensor_scalar(
+                out=res[t][0][:], in0=weighted[t][:], scalar1=factor[t][0][:], scalar2=0.0, op0=ALU.mult, op1=ALU.add
             )
+            store(t, 0, 0, HALF)
 
-        def finish_weighted(t, lo=0, hi=HALF):
+        def finish_on_scalar(t, lo, hi):
             nc.scalar.activation(
                 out=res[t][0][:, lo:hi], in_=weighted[t][:, lo:hi], func=ACT.Copy, scale=factor[t][0][:]
             )
-            nc.sync.dma_start(out=out[P * t : P * (t + 1), lo:hi], in_=res[t][0][:, lo:hi])
-
-        def casts(c):
-            for which in range(3):
-                cast(c, which)
-
-        def passes(c):
-            position_passes(c)
-            content_passes(c)
-
-        plane_loads = [
-            (plane, scales, r)
-            for plane, scales in ((qb_plane, qb_scales), (kb_plane, kb_scales), (qa_plane, qa_scales))
-            for r in range(4)
-        ]
-
-        def load_planes(engine, lo, hi):
-            for plane, scales, r in plane_loads[lo:hi]:
-                load_plane(engine, plane, scales, r)
+            store(t, 0, lo, hi)
 
         nc.vector.memset(qb_plane[:].bitcast(I32), 0)
         nc.vector.memset(kb_plane[:].bitcast(I32), 0)
         nc.gpsimd.memset(qa_plane[:].bitcast(I32), 0)
-        load_qa()
-        load_planes(nc.sync, 0, 5)
-        load_qb()
+
+        nc.sync.dma_start(out=qa_codes[:].bitcast(I32), in_=qa_words[0].rearrange("p n t -> p (n t)").bitcast(I32))
+        load_scales(nc.sync, scale_loads[:SCALE_LOADS_PER_ROUND])
+        nc.sync.dma_start(out=qb_codes[:].bitcast(I32), in_=qb_words[0].bitcast(I32))
         load_ka(0)
         load_kb(0)
-        load_planes(nc.sync, 5, 10)
-        load_planes(nc.gpsimd, 10, 12)
-        load_cw(nc.gpsimd)
+        load_scales(nc.sync, scale_loads[SCALE_LOADS_PER_ROUND : 2 * SCALE_LOADS_PER_ROUND])
+        load_scales(nc.gpsimd, scale_loads[2 * SCALE_LOADS_PER_ROUND :])
+        nc.gpsimd.dma_start(
+            out=cw_raw[:].rearrange("p (h j) -> p h j", j=PACK),
+            in_=cw1[0].rearrange("(h p j) -> p h j", h=2, j=PACK),
+        )
         make_identity(nc, ident[:])
-        scale_cw()
-        load_ka(1)
-        load_ka(2)
-        load_ka(3)
+        nc.gpsimd.tensor_scalar(
+            out=cw_cols[:], in0=cw_raw[:], scalar1=OUT_SCALE, scalar2=0.0, op0=ALU.mult, op1=ALU.add
+        )
+        for c in range(1, CHUNKS):
+            load_ka(c)
         load_kb(1)
 
-        def both(c, t):
-            position_passes(c, [t])
-            content_passes(c, [t])
-
-        casts(0)
+        round_chunk(0)
         quantize(0)
-        for t in range(TILES):
-            both(0, t)
+        chunk_scores(0)
         chunk_max(0, 0)
-        casts(1)
+        round_chunk(1)
         chunk_max(0, 1)
         quantize(1)
         chunk_max(0, 2)
         chunk_max(0, 3)
-        for t in range(TILES):
-            both(1, t)
-        casts(2)
+        chunk_scores(1)
+        spread_weights(0)
+        spread_weights(1)
+        round_chunk(2)
         chunk_max(1, 0)
         quantize(2)
+        first_max(0)
+        round_chunk(3)
         chunk_max(1, 1)
-        casts(3)
-        first_max(0, 2)
         quantize(3)
+        first_max(1)
+        first_exp(0)
+        nc.scalar.copy(out=by_word(first_weight[:]), in_=weight[0][:].rearrange("p j n -> p n j"))
+        weigh_first(0)
+        first_exp(1)
+        weigh_first(1)
         for t in range(TILES):
-            wide_position_pass(t)
-            content_passes(2, [t])
-            content_passes(3, [t])
-        exponentials(0, 0)
-        exponentials(1, 0)
-        spread(1, 0)
-        spread(0, 1)
+            second_scores(t)
         chunk_max(1, 2)
         chunk_max(1, 3)
-        first_max(2, 3)
-        exponentials(2, 0)
-        second_max(0)
-        first_max(3, TILES)
+        first_max(2)
+        first_exp(2)
+
+        row_max(0)
+        first_max(3)
         correction(0)
-        exponentials(0, 1)
-        second_max(1)
+        second_exp(0)
+        row_max(1)
         correction(1)
         denominator(0)
-        exponentials(1, 1)
-        second_max(2)
-        reciprocal(0)
-        second_max(3)
+        second_exp(1)
+        row_max(2)
+        second_factor(0)
         first_factor(0)
         correction(2)
         denominator(1)
-        exponentials(2, 1)
-        exponentials(3, 0)
+        second_exp(2)
+        finish(0, 1, 0, PIECE)
+        finish(0, 1, PIECE, HALF)
+        finish_on_gpsimd(0)
+
+        second_factor(1)
+        first_exp(3)
         denominator(2)
-        exponentials(3, 1)
-        denominator(3)
-        finish(0, 1)
-        reciprocal(1)
-        finish(0, 0)
+        row_max(3)
         first_factor(1)
+        correction(3)
+        second_exp(3)
+        denominator(3)
         finish(1, 1)
-        reciprocal(2)
-        finish(1, 0)
+        finish_on_gpsimd(1)
+        weigh_first(3)
+
+        second_factor(2)
         first_factor(2)
         finish(2, 1)
-        reciprocal(3)
+        second_factor(3)
         finish(2, 0)
+        first_factor(3)
         finish(3, 1)
-        finish(3, 0, 0, 256)
-        finish(3, 0, 256, 512)
+        finish_on_scalar(3, 0, PIECE)
+        finish_on_scalar(3, PIECE, HALF)

from contextlib import ExitStack

import concourse.mybir as mybir
from concourse.masks import make_identity

K, L, Q, I = 512, 512, 512, 1024
FLOPS = 2 * (K + L) * Q * I

F32 = mybir.dt.float32
BF16 = mybir.dt.bfloat16
I32 = mybir.dt.int32
U32 = mybir.dt.uint32
U8 = mybir.dt.uint8
FP8X4 = mybir.dt.float8_e4m3fn_x4
FP4X4 = mybir.dt.float4_e2m1fn_x4
ALU = mybir.AluOpType
ACT = mybir.ActivationFunctionType
AX = mybir.AxisListType

P = 128
PACK = 4
SCALE_ROWS = 16
QUADRANT = 32
TILES = Q // P
HALF = I // 2
CHUNK = 256
CHUNKS = I // CHUNK
NARROW = 128
PIECE = HALF // 2
OUT_SCALE = 256.0
VECTOR_COLUMNS = (168, 128, 128, 160)
SECOND_BANK = (4, 5, 0, 1)
WEIGHT_BANK = (6, 7)
SCALE_LOADS_PER_ROUND = 5


def tile_mix_shares_from_two_sources_kernel(
    tc, qa_words, qa_scales, ka, qb_words, qb_scales, kb_words, kb_scales, cw1, out
):
    nc = tc.nc
    with ExitStack() as ctx:
        keep = ctx.enter_context(tc.tile_pool(name="keep", bufs=1))
        psum = ctx.enter_context(tc.psum_pool(name="psum", bufs=1))
        ctx.enter_context(tc.manual_schedule())

        def sb(name, shape, dtype):
            return keep.tile(shape, dtype, name=name, align_bytes=64)

        def per_tile(name, width):
            return [sb("%s%d" % (name, t), [P, width], F32) for t in range(TILES)]

        def per_half(name, width):
            return [[sb("%s%d_%d" % (name, t, h), [P, width], F32) for h in range(2)] for t in range(TILES)]

        qa_plane = sb("qa_plane", [P, Q], U8)
        qb_plane = sb("qb_plane", [P, Q], U8)
        kb_plane = sb("kb_plane", [P, I], U8)
        qa_codes = sb("qa_codes", [P, Q], U32)
        qb_codes = sb("qb_codes", [P, 2 * Q], U8)
        kb_codes = [sb("kb_codes%d" % h, [P, HALF], U32) for h in range(2)]
        raw = [sb("raw%d" % c, [P, PACK, CHUNK], F32) for c in range(CHUNKS)]
        grouped = [sb("grouped%d" % c, [P, CHUNK * PACK], BF16) for c in range(CHUNKS)]
        ka_codes = [sb("ka_codes%d" % c, [P, CHUNK], U32) for c in range(CHUNKS)]
        ka_plane = [sb("ka_plane%d" % c, [P, CHUNK], U8) for c in range(CHUNKS)]
        cw_raw = sb("cw_raw", [P, 2 * PACK], F32)
        cw_cols = sb("cw_cols", [P, 2 * PACK], F32)
        first_weight = sb("first_weight", [P, HALF], F32)
        ident = sb("ident", [P, P], F32)
        neg_chunk = sb("neg_chunk", [P, TILES, 2], F32)
        neg_first = sb("neg_first", [P, TILES], F32)
        neg_row = per_tile("neg_row", 1)
        negated = per_tile("negated", HALF)
        sums = per_half("sum", 1)
        corr = per_tile("corr", 1)
        den = per_tile("den", 1)
        factor = per_half("factor", 1)
        expo = per_half("expo", HALF)
        res = per_half("res", HALF)
        weighted = {t: sb("weighted%d" % t, [P, HALF], F32) for t in (0, 1, 3)}
        score = [[psum.tile([P, HALF], F32, name="score%d_0" % t, tag="bank%d" % t), None] for t in range(TILES)]
        weight = [psum.tile([P, PACK, P], F32, name="weight%d" % h, tag="bank%d" % WEIGHT_BANK[h]) for h in range(2)]

        scale_loads = [
            (plane, scales, r)
            for plane, scales in ((qb_plane, qb_scales), (kb_plane, kb_scales), (qa_plane, qa_scales))
            for r in range(PACK)
        ]

        def load_scales(engine, loads):
            for plane, scales, r in loads:
                engine.dma_start(
                    out=plane[r:P:QUADRANT, :].bitcast(I32), in_=scales[0, r:SCALE_ROWS:PACK, :].bitcast(I32)
                )

        def load_ka(c):
            columns = ka[:, c * CHUNK : (c + 1) * CHUNK]
            nc.sync.dma_start(out=raw[c][:], in_=columns.rearrange("(p j) w -> p j w", j=PACK))

        def load_kb(h):
            rows = kb_words[0].rearrange("p n t -> p (n t)")
            nc.sync.dma_start(
                out=kb_codes[h][:].bitcast(I32), in_=rows[:, PACK * HALF * h : PACK * HALF * (h + 1)].bitcast(I32)
            )

        def round_chunk(c):
            split = VECTOR_COLUMNS[c]
            dst = grouped[c][:].rearrange("p (w t) -> p w t", t=PACK)
            src = raw[c][:].rearrange("p t w -> p w t")
            nc.vector.tensor_copy(out=dst[:, :split, :], in_=src[:, :split, :])
            nc.scalar.copy(out=dst[:, split:, :], in_=src[:, split:, :])

        def quantize(c):
            nc.vector.quantize_mx(out=ka_codes[c][:].bitcast(FP8X4), scales=ka_plane[c][:], in_=grouped[c][:])

        def position_pass(t, col, width, start):
            h, lo = divmod(col, HALF)
            nc.tensor.matmul_mx(
                out=score[t][h][:, lo : lo + width],
                lhsT=qb_codes[:, 2 * P * t : 2 * P * (t + 1)].bitcast(FP4X4),
                lhsT_scale=qb_plane[:, P * t : P * (t + 1)],
                rhs=kb_codes[h][:, lo : lo + width].bitcast(FP8X4),
                rhs_scale=kb_plane[:, col : col + width],
                start=start,
                stop=False,
            )

        def content_pass(t, c, stop):
            h, lo = divmod(c * CHUNK, HALF)
            nc.tensor.matmul_mx(
                out=score[t][h][:, lo : lo + CHUNK],
                lhsT=qa_codes[:, P * t : P * (t + 1)].bitcast(FP8X4),
                lhsT_scale=qa_plane[:, P * t : P * (t + 1)],
                rhs=ka_codes[c][:].bitcast(FP8X4),
                rhs_scale=ka_plane[c][:],
                start=False,
                stop=stop,
            )

        def chunk_scores(c):
            for t in range(TILES):
                for col in range(c * CHUNK, (c + 1) * CHUNK, NARROW):
                    position_pass(t, col, NARROW, start=(col == c * CHUNK))
                content_pass(t, c, stop=True)

        def second_scores(t):
            score[t][1] = psum.tile([P, HALF], F32, name="score%d_1" % t, tag="bank%d" % SECOND_BANK[t])
            position_pass(t, HALF, HALF, start=True)
            content_pass(t, 2, stop=False)
            content_pass(t, 3, stop=True)

        def spread_weights(h):
            for j in range(PACK):
                column = cw_cols[:, PACK * h + j : PACK * h + j + 1]
                nc.tensor.transpose(weight[h][:, j, :], column.to_broadcast([P, P]), ident[:])

        def by_word(ap):
            return ap.rearrange("p (n j) -> p n j", j=PACK)

        def chunk_max(c, t):
            nc.vector.tensor_reduce(
                out=neg_chunk[:, t, c : c + 1],
                in_=score[t][0][:, c * CHUNK : (c + 1) * CHUNK],
                axis=AX.X,
                op=ALU.max,
                negate=True,
            )

        def first_max(t):
            nc.vector.tensor_reduce(out=neg_first[:, t : t + 1], in_=neg_chunk[:, t : t + 1, :], axis=AX.X, op=ALU.min)

        def row_max(t):
            nc.vector.tensor_scalar(
                out=negated[t][:],
                in0=score[t][1][:],
                scalar1=-1.0,
                scalar2=neg_first[:, t : t + 1],
                op0=ALU.mult,
                op1=ALU.min,
                accum_out=neg_row[t][:],
            )

        def first_exp(t):
            nc.scalar.activation(
                out=expo[t][0][:],
                in_=score[t][0][:],
                func=ACT.Exp,
                bias=neg_first[:, t : t + 1],
                scale=1.0,
                accum_out=sums[t][0][:],
            )

        def second_exp(t):
            nc.scalar.activation(
                out=expo[t][1][:],
                in_=negated[t][:],
                func=ACT.Exp,
                bias=neg_row[t][:],
                scale=-1.0,
                accum_out=sums[t][1][:],
            )

        def correction(t):
            nc.scalar.activation(
                out=corr[t][:], in_=neg_first[:, t : t + 1], func=ACT.Exp, bias=neg_row[t][:], scale=-1.0
            )

        def denominator(t):
            nc.scalar.activation(
                out=den[t][:], in_=sums[t][0][:], func=ACT.Identity, bias=sums[t][1][:], scale=corr[t][:]
            )

        def second_factor(t):
            nc.vector.reciprocal(out=factor[t][1][:], in_=den[t][:])

        def first_factor(t):
            nc.vector.tensor_scalar(
                out=factor[t][0][:], in0=factor[t][1][:], scalar1=corr[t][:], scalar2=None, op0=ALU.mult
            )

        def store(t, h, lo, hi):
            nc.sync.dma_start(out=out[P * t : P * (t + 1), HALF * h + lo : HALF * h + hi], in_=res[t][h][:, lo:hi])

        def finish(t, h, lo=0, hi=HALF):
            nc.vector.scalar_tensor_tensor(
                out=by_word(res[t][h][:, lo:hi]),
                in0=by_word(expo[t][h][:, lo:hi]),
                scalar=factor[t][h][:],
                in1=weight[h][:, :, lo // PACK : hi // PACK].rearrange("p j n -> p n j"),
                op0=ALU.mult,
                op1=ALU.mult,
            )
            store(t, h, lo, hi)

        def weigh_first(t):
            nc.gpsimd.tensor_tensor(out=weighted[t][:], in0=expo[t][0][:], in1=first_weight[:], op=ALU.mult)

        def finish_on_gpsimd(t):
            nc.gpsimd.tensor_scalar(
                out=res[t][0][:], in0=weighted[t][:], scalar1=factor[t][0][:], scalar2=0.0, op0=ALU.mult, op1=ALU.add
            )
            store(t, 0, 0, HALF)

        def finish_on_scalar(t, lo, hi):
            nc.scalar.activation(
                out=res[t][0][:, lo:hi], in_=weighted[t][:, lo:hi], func=ACT.Copy, scale=factor[t][0][:]
            )
            store(t, 0, lo, hi)

        nc.vector.memset(qb_plane[:].bitcast(I32), 0)
        nc.vector.memset(kb_plane[:].bitcast(I32), 0)
        nc.gpsimd.memset(qa_plane[:].bitcast(I32), 0)

        nc.sync.dma_start(out=qa_codes[:].bitcast(I32), in_=qa_words[0].rearrange("p n t -> p (n t)").bitcast(I32))
        load_scales(nc.sync, scale_loads[:SCALE_LOADS_PER_ROUND])
        nc.sync.dma_start(out=qb_codes[:].bitcast(I32), in_=qb_words[0].bitcast(I32))
        load_ka(0)
        load_kb(0)
        load_scales(nc.sync, scale_loads[SCALE_LOADS_PER_ROUND : 2 * SCALE_LOADS_PER_ROUND])
        load_scales(nc.gpsimd, scale_loads[2 * SCALE_LOADS_PER_ROUND :])
        nc.gpsimd.dma_start(
            out=cw_raw[:].rearrange("p (h j) -> p h j", j=PACK),
            in_=cw1[0].rearrange("(h p j) -> p h j", h=2, j=PACK),
        )
        make_identity(nc, ident[:])
        nc.gpsimd.tensor_scalar(
            out=cw_cols[:], in0=cw_raw[:], scalar1=OUT_SCALE, scalar2=0.0, op0=ALU.mult, op1=ALU.add
        )
        for c in range(1, CHUNKS):
            load_ka(c)
        load_kb(1)

        round_chunk(0)
        quantize(0)
        chunk_scores(0)
        chunk_max(0, 0)
        round_chunk(1)
        chunk_max(0, 1)
        quantize(1)
        chunk_max(0, 2)
        chunk_max(0, 3)
        chunk_scores(1)
        spread_weights(0)
        spread_weights(1)
        round_chunk(2)
        chunk_max(1, 0)
        quantize(2)
        first_max(0)
        round_chunk(3)
        chunk_max(1, 1)
        quantize(3)
        first_max(1)
        first_exp(0)
        nc.scalar.copy(out=by_word(first_weight[:]), in_=weight[0][:].rearrange("p j n -> p n j"))
        weigh_first(0)
        first_exp(1)
        weigh_first(1)
        for t in range(TILES):
            second_scores(t)
        chunk_max(1, 2)
        chunk_max(1, 3)
        first_max(2)
        first_exp(2)

        row_max(0)
        first_max(3)
        correction(0)
        second_exp(0)
        row_max(1)
        correction(1)
        denominator(0)
        second_exp(1)
        row_max(2)
        second_factor(0)
        first_factor(0)
        correction(2)
        denominator(1)
        second_exp(2)
        finish(0, 1, 0, PIECE)
        finish(0, 1, PIECE, HALF)
        finish_on_gpsimd(0)

        second_factor(1)
        first_exp(3)
        denominator(2)
        row_max(3)
        first_factor(1)
        correction(3)
        second_exp(3)
        denominator(3)
        finish(1, 1)
        finish_on_gpsimd(1)
        weigh_first(3)

        second_factor(2)
        first_factor(2)
        finish(2, 1)
        second_factor(3)
        finish(2, 0)
        first_factor(3)
        finish(3, 1)
        finish_on_scalar(3, 0, PIECE)
        finish_on_scalar(3, PIECE, HALF)
